import numpy as np
CORES = [113,118,241,246]
N = 4
R, W, T = 4096, 16, 256
def entries(a): return a.T.reshape(-1)
def pack(v, P): return np.ascontiguousarray(np.asarray(v, np.int32).reshape(-1, P).T)
def lists(rng, how):
    Q = rng.permutation(N * R)[:N * T]
    if how == "hotrank": Q = R * int(rng.integers(N)) + rng.permutation(R)[:N * T]
    if how == "own": Q = np.concatenate([R * r + rng.permutation(R)[:T] for r in range(N)])
    if how == "sorted": Q = np.sort(Q)
    if how == "edge":
        ends = np.concatenate([R * np.arange(N), R * np.arange(N) + R - 1]); rest = np.setdiff1d(rng.permutation(N * R), ends, assume_unique=True)
        Q = rng.permutation(np.concatenate([ends, rng.permutation(rest)[:N * T - 2 * N]]))
    return {"pos": np.stack([pack(q, 128) for q in Q.reshape(N, T)])}
def setup_inputs(rng):
    return dict({"tab": rng.standard_normal((N, R, W), dtype=np.float32), "new": rng.standard_normal((N, T, W), dtype=np.float32)}, **lists(rng, "uniform"))
def setup_inputs_edge(rng):
    d = setup_inputs(rng); d.update(lists(rng, "edge"))
    for k in ("tab", "new"): d[k] = (d[k].astype(np.float32) * 1048576.0).astype(d[k].dtype)
    return d
def setup_inputs_hotrank(rng):
    d = setup_inputs(rng); d.update(lists(rng, "hotrank"))
    for k in ("tab", "new"): d[k] = (d[k].astype(np.float32) * (1 / 1024.0)).astype(d[k].dtype)
    return d
def setup_inputs_own(rng):
    d = setup_inputs(rng); d.update(lists(rng, "own"))
    return d
def setup_inputs_sorted(rng):
    d = setup_inputs(rng); d.update(lists(rng, "sorted"))
    return d
def check_inputs(x):
    bad = []
    if x["pos"].min() < 0 or x["pos"].max() >= N * R: bad.append("pos out of range")
    if len(np.unique(x["pos"])) != x["pos"].size: bad.append("a place is named twice")
    return bad
def reference(tab, new, pos):
    A = np.concatenate(list(tab), axis=0)
    for r in range(N): A[entries(pos[r])] = new[r]
    return {"y": np.stack([A[R * r:R * r + R] for r in range(N)])}

@@ -1,0 +1,185 @@
+from concourse.bass import DstId, RemoteDMATransfer
+from concourse.mybir import AluOpType as A, ActivationFunctionType as F
+
+N = 4
+WIN = 1536
+
+SCRATCH = {
+    "x": ("sbuf", [128, 512], "float32"),
+    "wnd": ("sbuf", [128, WIN], "float32"),
+    "gat": ("sbuf", [128, 512], "float32"),
+    "lnd": ("sbuf", [128, 144], "float32"),
+    "qi": ("sbuf", [128, 2], "int32"),
+    "kk4": ("sbuf", [128, 4], "int32"), "kf": ("sbuf", [128, 4], "float32"),
+    "ap": ("sbuf", [128, 2], "int32"), "ee": ("sbuf", [128, 2], "int32"),
+    "sd": ("sbuf", [128, 2], "int32"), "kr": ("sbuf", [128, 2], "int32"),
+    "ev": ("sbuf", [128, 2], "float32"), "tmp": ("sbuf", [128, 2], "float32"), "val": ("sbuf", [128, 2], "float32"),
+    "pidx": ("sbuf", [128, 1], "int32"), "pc": ("sbuf", [128, 3], "int32"), "pcf": ("sbuf", [128, 3], "float32"),
+    "rowa": ("sbuf", [128, 128], "float32"), "rowb": ("sbuf", [128, 128], "float32"),
+    "oha0": ("sbuf", [128, 128], "float16"), "oha1": ("sbuf", [128, 128], "float16"),
+    "ohb0": ("sbuf", [128, 128], "float16"), "ohb1": ("sbuf", [128, 128], "float16"),
+    "dsend": ("sbuf", [128, 128], "float32"),
+    "dland": ("sbuf", [128, 128], "float32"),
+    "ci0": ("sbuf", [128, 32], "float32"), "cio": ("sbuf", [128, 32], "float32"),
+    "m1": ("sbuf", [128, 64], "float32"), "m2": ("sbuf", [128, 32], "float32"),
+    "idx": ("sbuf", [128, 32], "uint16"),
+    "dmat": ("sbuf", [128, 128], "int32"), "pw": ("sbuf", [128, 224], "float32"),
+    "pr1": ("psum", [128, 512], "float32"), "pr2": ("psum", [128, 512], "float32"),
+    "pr3": ("psum", [128, 512], "float32"), "psd": ("psum", [128, 512], "float32"),
+}
+SEMAPHORES = (["ldpos", "ldnew", "ldtab", "cp", "cr", "cd", "cc", "k1", "k2", "i1", "i2", "i3", "i4", "i5", "oh", "mq", "ofd",
+               "p1", "p2", "q1", "q2", "dup", "tw", "fw", "x1", "x2", "x3", "gv", "ga", "bk", "st", "ls",
+               "r1", "r2", "r3"]
+              + ["va%d" % s for s in range(N)] + ["oa%d" % s for s in range(N)])
+
+
+def _take(allowed, used, n):
+    m = 0
+    for e in range(16):
+        b = 1 << e
+        if n and (allowed & b) and not (used & b):
+            m |= b
+            n -= 1
+    return m
+
+
+def rank_program(g, core, T, topo):
+    r = T.rank_of(core)
+    if r is None:
+        return
+    v, pe, act, sy, sem = g.vector, g.tensor, g.scalar, g.sync, T.sem
+    cores = T.cores
+    peers = [s for s in range(N) if s != r]
+    far = [s for s in peers if topo.same_plane(core, cores[s])]
+    far.sort(key=lambda s: topo.die(cores[s]) != topo.die(core))
+    near = [s for s in peers if s not in far]
+    NE = 4
+    masks, used = {}, 0
+    for s in far + near:
+        masks[s] = _take(topo.mask(core, cores[s]), used, NE)
+        used |= masks[s]
+
+    def send(src_of, dst, name):
+        trs = []
+        for s in far + near:
+            rid, pid = topo.addr(cores[s], core)
+            trs.append(RemoteDMATransfer(dst_ids=[DstId(rid=rid, pnc=pid)], dma_engine_mask=masks[s],
+                                         remote_sem=sem[name % r], src=src_of(s), dst=dst))
+        g.remote_dma_fused(trs, local_sem=sem.ls)
+
+    sy.dma_start(T.qi[:], T.pos[:]).then_inc(sem.ldpos, 16)
+    act.dma_start(T.lnd[:, 32 * r:32 * r + 16], T.new[0:128, :]).then_inc(sem.ldnew, 16)
+    sy.dma_start(T.lnd[:, 32 * r + 16:32 * r + 32], T.new[128:256, :]).then_inc(sem.ldnew, 16)
+    act.dma_start(T.x[:], T.tab[:]).then_inc(sem.ldtab, 16)
+
+    g.iota(T.pidx[:], [[0, 1]], 0, 1).then_inc(sem.cp, 1)
+    g.iota(T.rowa[:], [[1024, 4], [1, 2], [32, 16]], 0, 0, allow_small_or_imprecise_dtypes=True).then_inc(sem.cr, 1)
+    g.iota(T.rowb[:], [[4096, 4], [2, 16], [512, 2]], 0, 0, allow_small_or_imprecise_dtypes=True).then_inc(sem.cr, 1)
+    g.wait_ge(sem.ldnew, 32)
+    send(lambda s: T.lnd[:, 32 * r:32 * r + 32], T.lnd[:, 32 * r:32 * r + 32], "va%d")
+    g.iota(T.dmat[:], [[-1, 128]], 128, 1).then_inc(sem.cd, 1)
+    g.iota(T.ci0[:], [[16, 32]], 0, 1, allow_small_or_imprecise_dtypes=True).then_inc(sem.cc, 1)
+    g.wait_ge(sem.ofd, 1)
+    send(lambda s: T.dsend[:, 32 * s:32 * s + 32], T.dland[:, 32 * r:32 * r + 32], "oa%d")
+
+    v.wait_ge(sem.cp, 1)
+    v.tensor_scalar(out=T.pc[:, 0:1], in0=T.pidx[:], scalar1=5, scalar2=None, op0=A.logical_shift_right).then_inc(sem.k1, 1)
+    v.tensor_scalar(out=T.pc[:, 1:2], in0=T.pidx[:], scalar1=31, scalar2=None, op0=A.bitwise_and).then_inc(sem.k1, 1)
+    v.tensor_scalar(out=T.pc[:, 2:3], in0=T.pidx[:], scalar1=0x70, scalar2=None, op0=A.bitwise_and).then_inc(sem.k1, 1)
+    v.wait_ge(sem.k1, 3)
+    v.tensor_copy(out=T.pcf[:], in_=T.pc[:]).then_inc(sem.k2, 1)
+
+    v.wait_ge(sem.ldpos, 16)
+    v.tensor_scalar(out=T.kk4[:, 0:2], in0=T.qi[:], scalar1=0x0DE1, scalar2=None, op0=A.bitwise_and).then_inc(sem.i1, 1)
+    v.tensor_scalar(out=T.kk4[:, 2:4], in0=T.qi[:], scalar1=0x321E, scalar2=None, op0=A.bitwise_and).then_inc(sem.i1, 1)
+    v.tensor_scalar(out=T.ap[:], in0=T.qi[:], scalar1=10, scalar2=3, op0=A.logical_shift_right,
+                    op1=A.bitwise_and).then_inc(sem.i1, 1)
+    v.tensor_scalar(out=T.ee[:], in0=T.qi[:], scalar1=1, scalar2=None, op0=A.bitwise_and).then_inc(sem.i1, 1)
+    v.wait_ge(sem.i1, 4)
+    v.wait_ge(sem.k2, 1)
+    b1 = (r + 3) % N
+    v.tensor_scalar(out=T.sd[:], in0=T.ap[:], scalar1=T.pcf[:, 0:1], scalar2=4, op0=A.subtract, op1=A.add).then_inc(sem.i2, 1)
+    v.tensor_copy(out=T.kf[:], in_=T.kk4[:]).then_inc(sem.i2, 1)
+    v.tensor_scalar(out=T.ev[:, 0:1], in0=T.ee[:, 0:1], scalar1=128 + 32 * b1 - 32 * r, scalar2=512 + 32 * r, op0=A.mult,
+                    op1=A.add).then_inc(sem.i2, 1)
+    v.tensor_scalar(out=T.ev[:, 1:2], in0=T.ee[:, 1:2], scalar1=-128, scalar2=512 + 128 + 32 * r, op0=A.mult,
+                    op1=A.add).then_inc(sem.i2, 1)
+    v.wait_ge(sem.i2, 4)
+    v.tensor_scalar(out=T.kr[:], in0=T.sd[:], scalar1=3, scalar2=None, op0=A.bitwise_and).then_inc(sem.i3, 1)
+    v.wait_ge(sem.cr, 2)
+    v.tensor_scalar(out=T.oha0[:], in0=T.rowa[:], scalar1=T.kf[:, 0:1], scalar2=None, op0=A.is_equal).then_inc(sem.oh, 1)
+    v.wait_ge(sem.i3, 1)
+    v.tensor_scalar(out=T.tmp[:], in0=T.kr[:], scalar1=256, scalar2=T.pcf[:, 1:2], op0=A.mult, op1=A.add).then_inc(sem.i4, 1)
+    v.tensor_scalar(out=T.oha1[:], in0=T.rowa[:], scalar1=T.kf[:, 1:2], scalar2=None, op0=A.is_equal).then_inc(sem.oh, 1)
+    v.wait_ge(sem.i4, 1)
+    v.tensor_tensor(out=T.val[:], in0=T.tmp[:], in1=T.ev[:], op=A.add).then_inc(sem.i5, 1)
+    v.wait_ge(sem.i5, 1)
+    v.tensor_scalar(out=T.ohb0[:], in0=T.rowb[:], scalar1=T.kf[:, 2:3], scalar2=T.val[:, 0:1], op0=A.is_equal,
+                    op1=A.mult).then_inc(sem.oh, 1)
+    v.tensor_scalar(out=T.ohb1[:], in0=T.rowb[:], scalar1=T.kf[:, 3:4], scalar2=T.val[:, 1:2], op0=A.is_equal,
+                    op1=A.mult).then_inc(sem.oh, 1)
+    pe.wait_ge(sem.oh, 4)
+    pe.matmul(T.psd[:, 0:128], T.oha0[:], T.ohb0[:], True, False)
+    pe.matmul(T.psd[:, 0:128], T.oha1[:], T.ohb1[:], False, True).then_inc(sem.mq, 1)
+    v.wait_ge(sem.mq, 1)
+    v.tensor_copy(out=T.dsend[:], in_=T.psd[:, 0:128]).then_inc(sem.ofd, 1)
+
+    v.wait_ge(sem.cd, 1)
+    v.tensor_scalar(out=T.pw[:, 0:128], in0=T.dmat[:], scalar1=128, scalar2=None, op0=A.is_equal).then_inc(sem.p1, 1)
+    v.wait_ge(sem.p1, 1)
+    v.tensor_copy(out=T.pw[:, 128:224], in_=T.pw[:, 0:96]).then_inc(sem.p2, 1)
+    v.wait_ge(sem.cc, 1)
+    v.tensor_scalar(out=T.cio[:], in0=T.ci0[:], scalar1=T.pcf[:, 2:3], scalar2=None, op0=A.subtract).then_inc(sem.q1, 1)
+    v.wait_ge(sem.q1, 1)
+    v.wait_ge(sem.ofd, 1)
+    v.tensor_tensor(out=T.dland[:, 32 * r:32 * r + 32], in0=T.dsend[:, 32 * r:32 * r + 32], in1=T.cio[:],
+                    op=A.max).then_inc(sem.q2, 1)
+
+    v.wait_ge(sem.ldnew, 32)
+    for s in near + far:
+        v.wait_ge(sem["va%d" % s], NE)
+    v.tensor_copy(out=T.lnd[:, 128:144], in_=T.lnd[:, 0:16]).then_inc(sem.dup, 1)
+    pe.wait_ge(sem.ldnew, 32)
+    for s in near + far:
+        pe.wait_ge(sem["va%d" % s], NE)
+    pe.wait_ge(sem.p1, 1)
+    pe.wait_ge(sem.p2, 1)
+    pe.wait_ge(sem.dup, 1)
+    for k in (1, 2, 3):
+        pe.matmul(T["pr%d" % k][:, 0:144], T.pw[:, 128 - 32 * k:256 - 32 * k], T.lnd[:], True, True).then_inc(sem["r%d" % k], 1)
+    v.wait_ge(sem.dup, 1)
+    v.transpose(out=T.wnd[:, 512:640], in_=T.lnd[:, 0:128]).then_inc(sem.tw, 1)
+    v.transpose(out=T.wnd[:, 640:768], in_=T.lnd[:, 16:144]).then_inc(sem.tw, 1)
+    v.wait_ge(sem.ldtab, 16)
+    v.transpose(out=T.wnd[:, 0:512], in_=T.x[:]).then_inc(sem.fw, 1)
+    for k in (1, 2, 3):
+        c0 = 512 + 256 * k
+        v.wait_ge(sem["r%d" % k], 1)
+        v.transpose(out=T.wnd[:, c0:c0 + 128], in_=T["pr%d" % k][:, 0:128]).then_inc(sem.tw, 1)
+        v.transpose(out=T.wnd[:, c0 + 128:c0 + 256], in_=T["pr%d" % k][:, 16:144]).then_inc(sem.tw, 1)
+
+    v.wait_ge(sem.q2, 1)
+    for s in near + far:
+        v.wait_ge(sem["oa%d" % s], NE)
+    v.tensor_tensor(out=T.m1[:], in0=T.dland[:, 0:64], in1=T.dland[:, 64:128], op=A.max).then_inc(sem.x1, 1)
+    v.wait_ge(sem.x1, 1)
+    v.tensor_tensor(out=T.m2[:], in0=T.m1[:, 0:32], in1=T.m1[:, 32:64], op=A.max).then_inc(sem.x2, 1)
+    v.wait_ge(sem.x2, 1)
+    v.tensor_copy(out=T.idx[:], in_=T.m2[:]).then_inc(sem.x3, 1)
+
+    act.wait_ge(sem.tw, 8)
+    act.wait_ge(sem.fw, 1)
+    act.wait_ge(sem.x3, 1)
+    act.activation(T.gat[:, 256:512], T.wnd[:, 0:WIN].indirect(T.idx[:, 16:32]), F.Copy).then_inc(sem.ga, 1)
+    v.wait_ge(sem.tw, 8)
+    v.wait_ge(sem.fw, 1)
+    v.wait_ge(sem.x3, 1)
+    v.tensor_copy(out=T.gat[:, 0:256], in_=T.wnd[:, 0:WIN].indirect(T.idx[:, 0:16])).then_inc(sem.gv, 1)
+    v.wait_ge(sem.gv, 1)
+    v.transpose(out=T.x[:, 0:256], in_=T.gat[:, 0:256]).then_inc(sem.bk, 1)
+    v.wait_ge(sem.ga, 1)
+    v.transpose(out=T.x[:, 256:512], in_=T.gat[:, 256:512]).then_inc(sem.bk, 1)
+    sy.wait_ge(sem.bk, 2)
+    sy.dma_start(T.y[:], T.x[:]).then_inc(sem.st, 16)
+    sy.wait_ge(sem.st, 16)
+    g.wait_ge(sem.ls, 2 * 3 * NE)

@@ -2,6 +2,7 @@ from concourse.bass import DstId, RemoteDMATransfer
 from concourse.mybir import AluOpType as A, ActivationFunctionType as F
 
 N = 4
+H = 4
 WIN = 1536
 
 SCRATCH = {
@@ -28,8 +29,9 @@ SCRATCH = {
     "pr3": ("psum", [128, 512], "float32"), "psd": ("psum", [128, 512], "float32"),
 }
 SEMAPHORES = (["ldpos", "ldnew", "ldtab", "cp", "cr", "cd", "cc", "k1", "k2", "i1", "i2", "i3", "i4", "i5", "oh", "mq", "ofd",
-               "p1", "p2", "q1", "q2", "dup", "tw", "fw", "x1", "x2", "x3", "gv", "ga", "bk", "st", "ls",
+               "p1", "p2", "q1", "q2", "dup", "tw", "fw", "x1", "x2", "x3", "st", "stl", "ls",
                "r1", "r2", "r3"]
+              + ["ga%d" % h for h in range(H)] + ["bk%d" % h for h in range(H)]
               + ["va%d" % s for s in range(N)] + ["oa%d" % s for s in range(N)])
 
 
@@ -70,11 +72,13 @@ def rank_program(g, core, T, topo):
     sy.dma_start(T.qi[:], T.pos[:]).then_inc(sem.ldpos, 16)
     act.dma_start(T.lnd[:, 32 * r:32 * r + 16], T.new[0:128, :]).then_inc(sem.ldnew, 16)
     sy.dma_start(T.lnd[:, 32 * r + 16:32 * r + 32], T.new[128:256, :]).then_inc(sem.ldnew, 16)
-    act.dma_start(T.x[:], T.tab[:]).then_inc(sem.ldtab, 16)
+    for h in range(H):
+        (act if h % 2 == 0 else sy).dma_start(T.x[:, 128 * h:128 * h + 128],
+                                              T.tab[1024 * h:1024 * h + 1024, :]).then_inc(sem.ldtab, 16)
 
     g.iota(T.pidx[:], [[0, 1]], 0, 1).then_inc(sem.cp, 1)
-    g.iota(T.rowa[:], [[1024, 4], [1, 2], [32, 16]], 0, 0, allow_small_or_imprecise_dtypes=True).then_inc(sem.cr, 1)
-    g.iota(T.rowb[:], [[4096, 4], [2, 16], [512, 2]], 0, 0, allow_small_or_imprecise_dtypes=True).then_inc(sem.cr, 1)
+    g.iota(T.rowa[:], [[256, 4], [1, 2], [8, 16]], 0, 0, allow_small_or_imprecise_dtypes=True).then_inc(sem.cr, 1)
+    g.iota(T.rowb[:], [[1024, 16], [2, 4], [128, 2]], 0, 0, allow_small_or_imprecise_dtypes=True).then_inc(sem.cr, 1)
     g.wait_ge(sem.ldnew, 32)
     send(lambda s: T.lnd[:, 32 * r:32 * r + 32], T.lnd[:, 32 * r:32 * r + 32], "va%d")
     g.iota(T.dmat[:], [[-1, 128]], 128, 1).then_inc(sem.cd, 1)
@@ -90,9 +94,9 @@ def rank_program(g, core, T, topo):
     v.tensor_copy(out=T.pcf[:], in_=T.pc[:]).then_inc(sem.k2, 1)
 
     v.wait_ge(sem.ldpos, 16)
-    v.tensor_scalar(out=T.kk4[:, 0:2], in0=T.qi[:], scalar1=0x0DE1, scalar2=None, op0=A.bitwise_and).then_inc(sem.i1, 1)
-    v.tensor_scalar(out=T.kk4[:, 2:4], in0=T.qi[:], scalar1=0x321E, scalar2=None, op0=A.bitwise_and).then_inc(sem.i1, 1)
-    v.tensor_scalar(out=T.ap[:], in0=T.qi[:], scalar1=10, scalar2=3, op0=A.logical_shift_right,
+    v.tensor_scalar(out=T.kk4[:, 0:2], in0=T.qi[:], scalar1=0x0379, scalar2=None, op0=A.bitwise_and).then_inc(sem.i1, 1)
+    v.tensor_scalar(out=T.kk4[:, 2:4], in0=T.qi[:], scalar1=0x3C86, scalar2=None, op0=A.bitwise_and).then_inc(sem.i1, 1)
+    v.tensor_scalar(out=T.ap[:], in0=T.qi[:], scalar1=8, scalar2=3, op0=A.logical_shift_right,
                     op1=A.bitwise_and).then_inc(sem.i1, 1)
     v.tensor_scalar(out=T.ee[:], in0=T.qi[:], scalar1=1, scalar2=None, op0=A.bitwise_and).then_inc(sem.i1, 1)
     v.wait_ge(sem.i1, 4)
@@ -135,10 +139,12 @@ def rank_program(g, core, T, topo):
     v.tensor_tensor(out=T.dland[:, 32 * r:32 * r + 32], in0=T.dsend[:, 32 * r:32 * r + 32], in1=T.cio[:],
                     op=A.max).then_inc(sem.q2, 1)
 
-    v.wait_ge(sem.ldnew, 32)
-    for s in near + far:
-        v.wait_ge(sem["va%d" % s], NE)
-    v.tensor_copy(out=T.lnd[:, 128:144], in_=T.lnd[:, 0:16]).then_inc(sem.dup, 1)
+    if r == 0:
+        act.wait_ge(sem.ldnew, 32)
+    else:
+        act.wait_ge(sem.va0, NE)
+    act.activation(T.lnd[:, 128:144], T.lnd[:, 0:16], F.Copy).then_inc(sem.dup, 1)
+
     pe.wait_ge(sem.ldnew, 32)
     for s in near + far:
         pe.wait_ge(sem["va%d" % s], NE)
@@ -147,10 +153,13 @@ def rank_program(g, core, T, topo):
     pe.wait_ge(sem.dup, 1)
     for k in (1, 2, 3):
         pe.matmul(T["pr%d" % k][:, 0:144], T.pw[:, 128 - 32 * k:256 - 32 * k], T.lnd[:], True, True).then_inc(sem["r%d" % k], 1)
-    v.wait_ge(sem.dup, 1)
+    v.wait_ge(sem.ldnew, 32)
+    for s in near + far:
+        v.wait_ge(sem["va%d" % s], NE)
     v.transpose(out=T.wnd[:, 512:640], in_=T.lnd[:, 0:128]).then_inc(sem.tw, 1)
+    v.wait_ge(sem.dup, 1)
     v.transpose(out=T.wnd[:, 640:768], in_=T.lnd[:, 16:144]).then_inc(sem.tw, 1)
-    v.wait_ge(sem.ldtab, 16)
+    v.wait_ge(sem.ldtab, 16 * H)
     v.transpose(out=T.wnd[:, 0:512], in_=T.x[:]).then_inc(sem.fw, 1)
     for k in (1, 2, 3):
         c0 = 512 + 256 * k
@@ -167,19 +176,27 @@ def rank_program(g, core, T, topo):
     v.wait_ge(sem.x2, 1)
     v.tensor_copy(out=T.idx[:], in_=T.m2[:]).then_inc(sem.x3, 1)
 
+    def piece(h):
+        return T.wnd[:, 0:WIN].indirect(T.idx[:, 8 * h:8 * h + 8])
+
     act.wait_ge(sem.tw, 8)
     act.wait_ge(sem.fw, 1)
     act.wait_ge(sem.x3, 1)
-    act.activation(T.gat[:, 256:512], T.wnd[:, 0:WIN].indirect(T.idx[:, 16:32]), F.Copy).then_inc(sem.ga, 1)
+    for h in range(1, H):
+        act.activation(T.gat[:, 128 * h:128 * h + 128], piece(h), F.Copy).then_inc(sem["ga%d" % h], 1)
     v.wait_ge(sem.tw, 8)
     v.wait_ge(sem.fw, 1)
     v.wait_ge(sem.x3, 1)
-    v.tensor_copy(out=T.gat[:, 0:256], in_=T.wnd[:, 0:WIN].indirect(T.idx[:, 0:16])).then_inc(sem.gv, 1)
-    v.wait_ge(sem.gv, 1)
-    v.transpose(out=T.x[:, 0:256], in_=T.gat[:, 0:256]).then_inc(sem.bk, 1)
-    v.wait_ge(sem.ga, 1)
-    v.transpose(out=T.x[:, 256:512], in_=T.gat[:, 256:512]).then_inc(sem.bk, 1)
-    sy.wait_ge(sem.bk, 2)
-    sy.dma_start(T.y[:], T.x[:]).then_inc(sem.st, 16)
-    sy.wait_ge(sem.st, 16)
+    v.tensor_copy(out=T.gat[:, 0:128], in_=piece(0)).then_inc(sem.ga0, 1)
+    for h in range(H):
+        v.wait_ge(sem["ga%d" % h], 1)
+        v.transpose(out=T.x[:, 128 * h:128 * h + 128], in_=T.gat[:, 128 * h:128 * h + 128]).then_inc(sem["bk%d" % h], 1)
+    for h in range(H - 1):
+        sy.wait_ge(sem["bk%d" % h], 1)
+        sy.dma_start(T.y[1024 * h:1024 * h + 1024, :], T.x[:, 128 * h:128 * h + 128]).then_inc(sem.st, 16)
+    h = H - 1
+    act.wait_ge(sem["bk%d" % h], 1)
+    act.dma_start(T.y[1024 * h:1024 * h + 1024, :], T.x[:, 128 * h:128 * h + 128]).then_inc(sem.stl, 16)
+    sy.wait_ge(sem.st, 16 * (H - 1))
+    act.wait_ge(sem.stl, 16)
     g.wait_ge(sem.ls, 2 * 3 * NE)

from concourse.bass import DstId, RemoteDMATransfer
from concourse.mybir import AluOpType as A, ActivationFunctionType as F

N = 4
H = 4
WIN = 1536

SCRATCH = {
    "x": ("sbuf", [128, 512], "float32"),
    "wnd": ("sbuf", [128, WIN], "float32"),
    "gat": ("sbuf", [128, 512], "float32"),
    "lnd": ("sbuf", [128, 144], "float32"),
    "qi": ("sbuf", [128, 2], "int32"),
    "kk4": ("sbuf", [128, 4], "int32"), "kf": ("sbuf", [128, 4], "float32"),
    "ap": ("sbuf", [128, 2], "int32"), "ee": ("sbuf", [128, 2], "int32"),
    "sd": ("sbuf", [128, 2], "int32"), "kr": ("sbuf", [128, 2], "int32"),
    "ev": ("sbuf", [128, 2], "float32"), "tmp": ("sbuf", [128, 2], "float32"), "val": ("sbuf", [128, 2], "float32"),
    "pidx": ("sbuf", [128, 1], "int32"), "pc": ("sbuf", [128, 3], "int32"), "pcf": ("sbuf", [128, 3], "float32"),
    "rowa": ("sbuf", [128, 128], "float32"), "rowb": ("sbuf", [128, 128], "float32"),
    "oha0": ("sbuf", [128, 128], "float16"), "oha1": ("sbuf", [128, 128], "float16"),
    "ohb0": ("sbuf", [128, 128], "float16"), "ohb1": ("sbuf", [128, 128], "float16"),
    "dsend": ("sbuf", [128, 128], "float32"),
    "dland": ("sbuf", [128, 128], "float32"),
    "ci0": ("sbuf", [128, 32], "float32"), "cio": ("sbuf", [128, 32], "float32"),
    "m1": ("sbuf", [128, 64], "float32"), "m2": ("sbuf", [128, 32], "float32"),
    "idx": ("sbuf", [128, 32], "uint16"),
    "dmat": ("sbuf", [128, 128], "int32"), "pw": ("sbuf", [128, 224], "float32"),
    "pr1": ("psum", [128, 512], "float32"), "pr2": ("psum", [128, 512], "float32"),
    "pr3": ("psum", [128, 512], "float32"), "psd": ("psum", [128, 512], "float32"),
}
SEMAPHORES = (["ldpos", "ldnew", "ldtab", "cp", "cr", "cd", "cc", "k1", "k2", "i1", "i2", "i3", "i4", "i5", "oh", "mq", "ofd",
               "p1", "p2", "q1", "q2", "dup", "tw", "fw", "x1", "x2", "x3", "st", "stl", "ls",
               "r1", "r2", "r3"]
              + ["ga%d" % h for h in range(H)] + ["bk%d" % h for h in range(H)]
              + ["va%d" % s for s in range(N)] + ["oa%d" % s for s in range(N)])


def _take(allowed, used, n):
    m = 0
    for e in range(16):
        b = 1 << e
        if n and (allowed & b) and not (used & b):
            m |= b
            n -= 1
    return m


def rank_program(g, core, T, topo):
    r = T.rank_of(core)
    if r is None:
        return
    v, pe, act, sy, sem = g.vector, g.tensor, g.scalar, g.sync, T.sem
    cores = T.cores
    peers = [s for s in range(N) if s != r]
    far = [s for s in peers if topo.same_plane(core, cores[s])]
    far.sort(key=lambda s: topo.die(cores[s]) != topo.die(core))
    near = [s for s in peers if s not in far]
    NE = 4
    masks, used = {}, 0
    for s in far + near:
        masks[s] = _take(topo.mask(core, cores[s]), used, NE)
        used |= masks[s]

    def send(src_of, dst, name):
        trs = []
        for s in far + near:
            rid, pid = topo.addr(cores[s], core)
            trs.append(RemoteDMATransfer(dst_ids=[DstId(rid=rid, pnc=pid)], dma_engine_mask=masks[s],
                                         remote_sem=sem[name % r], src=src_of(s), dst=dst))
        g.remote_dma_fused(trs, local_sem=sem.ls)

    sy.dma_start(T.qi[:], T.pos[:]).then_inc(sem.ldpos, 16)
    act.dma_start(T.lnd[:, 32 * r:32 * r + 16], T.new[0:128, :]).then_inc(sem.ldnew, 16)
    sy.dma_start(T.lnd[:, 32 * r + 16:32 * r + 32], T.new[128:256, :]).then_inc(sem.ldnew, 16)
    for h in range(H):
        (act if h % 2 == 0 else sy).dma_start(T.x[:, 128 * h:128 * h + 128],
                                              T.tab[1024 * h:1024 * h + 1024, :]).then_inc(sem.ldtab, 16)

    g.iota(T.pidx[:], [[0, 1]], 0, 1).then_inc(sem.cp, 1)
    g.iota(T.rowa[:], [[256, 4], [1, 2], [8, 16]], 0, 0, allow_small_or_imprecise_dtypes=True).then_inc(sem.cr, 1)
    g.iota(T.rowb[:], [[1024, 16], [2, 4], [128, 2]], 0, 0, allow_small_or_imprecise_dtypes=True).then_inc(sem.cr, 1)
    g.wait_ge(sem.ldnew, 32)
    send(lambda s: T.lnd[:, 32 * r:32 * r + 32], T.lnd[:, 32 * r:32 * r + 32], "va%d")
    g.iota(T.dmat[:], [[-1, 128]], 128, 1).then_inc(sem.cd, 1)
    g.iota(T.ci0[:], [[16, 32]], 0, 1, allow_small_or_imprecise_dtypes=True).then_inc(sem.cc, 1)
    g.wait_ge(sem.ofd, 1)
    send(lambda s: T.dsend[:, 32 * s:32 * s + 32], T.dland[:, 32 * r:32 * r + 32], "oa%d")

    v.wait_ge(sem.cp, 1)
    v.tensor_scalar(out=T.pc[:, 0:1], in0=T.pidx[:], scalar1=5, scalar2=None, op0=A.logical_shift_right).then_inc(sem.k1, 1)
    v.tensor_scalar(out=T.pc[:, 1:2], in0=T.pidx[:], scalar1=31, scalar2=None, op0=A.bitwise_and).then_inc(sem.k1, 1)
    v.tensor_scalar(out=T.pc[:, 2:3], in0=T.pidx[:], scalar1=0x70, scalar2=None, op0=A.bitwise_and).then_inc(sem.k1, 1)
    v.wait_ge(sem.k1, 3)
    v.tensor_copy(out=T.pcf[:], in_=T.pc[:]).then_inc(sem.k2, 1)

    v.wait_ge(sem.ldpos, 16)
    v.tensor_scalar(out=T.kk4[:, 0:2], in0=T.qi[:], scalar1=0x0379, scalar2=None, op0=A.bitwise_and).then_inc(sem.i1, 1)
    v.tensor_scalar(out=T.kk4[:, 2:4], in0=T.qi[:], scalar1=0x3C86, scalar2=None, op0=A.bitwise_and).then_inc(sem.i1, 1)
    v.tensor_scalar(out=T.ap[:], in0=T.qi[:], scalar1=8, scalar2=3, op0=A.logical_shift_right,
                    op1=A.bitwise_and).then_inc(sem.i1, 1)
    v.tensor_scalar(out=T.ee[:], in0=T.qi[:], scalar1=1, scalar2=None, op0=A.bitwise_and).then_inc(sem.i1, 1)
    v.wait_ge(sem.i1, 4)
    v.wait_ge(sem.k2, 1)
    b1 = (r + 3) % N
    v.tensor_scalar(out=T.sd[:], in0=T.ap[:], scalar1=T.pcf[:, 0:1], scalar2=4, op0=A.subtract, op1=A.add).then_inc(sem.i2, 1)
    v.tensor_copy(out=T.kf[:], in_=T.kk4[:]).then_inc(sem.i2, 1)
    v.tensor_scalar(out=T.ev[:, 0:1], in0=T.ee[:, 0:1], scalar1=128 + 32 * b1 - 32 * r, scalar2=512 + 32 * r, op0=A.mult,
                    op1=A.add).then_inc(sem.i2, 1)
    v.tensor_scalar(out=T.ev[:, 1:2], in0=T.ee[:, 1:2], scalar1=-128, scalar2=512 + 128 + 32 * r, op0=A.mult,
                    op1=A.add).then_inc(sem.i2, 1)
    v.wait_ge(sem.i2, 4)
    v.tensor_scalar(out=T.kr[:], in0=T.sd[:], scalar1=3, scalar2=None, op0=A.bitwise_and).then_inc(sem.i3, 1)
    v.wait_ge(sem.cr, 2)
    v.tensor_scalar(out=T.oha0[:], in0=T.rowa[:], scalar1=T.kf[:, 0:1], scalar2=None, op0=A.is_equal).then_inc(sem.oh, 1)
    v.wait_ge(sem.i3, 1)
    v.tensor_scalar(out=T.tmp[:], in0=T.kr[:], scalar1=256, scalar2=T.pcf[:, 1:2], op0=A.mult, op1=A.add).then_inc(sem.i4, 1)
    v.tensor_scalar(out=T.oha1[:], in0=T.rowa[:], scalar1=T.kf[:, 1:2], scalar2=None, op0=A.is_equal).then_inc(sem.oh, 1)
    v.wait_ge(sem.i4, 1)
    v.tensor_tensor(out=T.val[:], in0=T.tmp[:], in1=T.ev[:], op=A.add).then_inc(sem.i5, 1)
    v.wait_ge(sem.i5, 1)
    v.tensor_scalar(out=T.ohb0[:], in0=T.rowb[:], scalar1=T.kf[:, 2:3], scalar2=T.val[:, 0:1], op0=A.is_equal,
                    op1=A.mult).then_inc(sem.oh, 1)
    v.tensor_scalar(out=T.ohb1[:], in0=T.rowb[:], scalar1=T.kf[:, 3:4], scalar2=T.val[:, 1:2], op0=A.is_equal,
                    op1=A.mult).then_inc(sem.oh, 1)
    pe.wait_ge(sem.oh, 4)
    pe.matmul(T.psd[:, 0:128], T.oha0[:], T.ohb0[:], True, False)
    pe.matmul(T.psd[:, 0:128], T.oha1[:], T.ohb1[:], False, True).then_inc(sem.mq, 1)
    v.wait_ge(sem.mq, 1)
    v.tensor_copy(out=T.dsend[:], in_=T.psd[:, 0:128]).then_inc(sem.ofd, 1)

    v.wait_ge(sem.cd, 1)
    v.tensor_scalar(out=T.pw[:, 0:128], in0=T.dmat[:], scalar1=128, scalar2=None, op0=A.is_equal).then_inc(sem.p1, 1)
    v.wait_ge(sem.p1, 1)
    v.tensor_copy(out=T.pw[:, 128:224], in_=T.pw[:, 0:96]).then_inc(sem.p2, 1)
    v.wait_ge(sem.cc, 1)
    v.tensor_scalar(out=T.cio[:], in0=T.ci0[:], scalar1=T.pcf[:, 2:3], scalar2=None, op0=A.subtract).then_inc(sem.q1, 1)
    v.wait_ge(sem.q1, 1)
    v.wait_ge(sem.ofd, 1)
    v.tensor_tensor(out=T.dland[:, 32 * r:32 * r + 32], in0=T.dsend[:, 32 * r:32 * r + 32], in1=T.cio[:],
                    op=A.max).then_inc(sem.q2, 1)

    if r == 0:
        act.wait_ge(sem.ldnew, 32)
    else:
        act.wait_ge(sem.va0, NE)
    act.activation(T.lnd[:, 128:144], T.lnd[:, 0:16], F.Copy).then_inc(sem.dup, 1)

    pe.wait_ge(sem.ldnew, 32)
    for s in near + far:
        pe.wait_ge(sem["va%d" % s], NE)
    pe.wait_ge(sem.p1, 1)
    pe.wait_ge(sem.p2, 1)
    pe.wait_ge(sem.dup, 1)
    for k in (1, 2, 3):
        pe.matmul(T["pr%d" % k][:, 0:144], T.pw[:, 128 - 32 * k:256 - 32 * k], T.lnd[:], True, True).then_inc(sem["r%d" % k], 1)
    v.wait_ge(sem.ldnew, 32)
    for s in near + far:
        v.wait_ge(sem["va%d" % s], NE)
    v.transpose(out=T.wnd[:, 512:640], in_=T.lnd[:, 0:128]).then_inc(sem.tw, 1)
    v.wait_ge(sem.dup, 1)
    v.transpose(out=T.wnd[:, 640:768], in_=T.lnd[:, 16:144]).then_inc(sem.tw, 1)
    v.wait_ge(sem.ldtab, 16 * H)
    v.transpose(out=T.wnd[:, 0:512], in_=T.x[:]).then_inc(sem.fw, 1)
    for k in (1, 2, 3):
        c0 = 512 + 256 * k
        v.wait_ge(sem["r%d" % k], 1)
        v.transpose(out=T.wnd[:, c0:c0 + 128], in_=T["pr%d" % k][:, 0:128]).then_inc(sem.tw, 1)
        v.transpose(out=T.wnd[:, c0 + 128:c0 + 256], in_=T["pr%d" % k][:, 16:144]).then_inc(sem.tw, 1)

    v.wait_ge(sem.q2, 1)
    for s in near + far:
        v.wait_ge(sem["oa%d" % s], NE)
    v.tensor_tensor(out=T.m1[:], in0=T.dland[:, 0:64], in1=T.dland[:, 64:128], op=A.max).then_inc(sem.x1, 1)
    v.wait_ge(sem.x1, 1)
    v.tensor_tensor(out=T.m2[:], in0=T.m1[:, 0:32], in1=T.m1[:, 32:64], op=A.max).then_inc(sem.x2, 1)
    v.wait_ge(sem.x2, 1)
    v.tensor_copy(out=T.idx[:], in_=T.m2[:]).then_inc(sem.x3, 1)

    def piece(h):
        return T.wnd[:, 0:WIN].indirect(T.idx[:, 8 * h:8 * h + 8])

    act.wait_ge(sem.tw, 8)
    act.wait_ge(sem.fw, 1)
    act.wait_ge(sem.x3, 1)
    for h in range(1, H):
        act.activation(T.gat[:, 128 * h:128 * h + 128], piece(h), F.Copy).then_inc(sem["ga%d" % h], 1)
    v.wait_ge(sem.tw, 8)
    v.wait_ge(sem.fw, 1)
    v.wait_ge(sem.x3, 1)
    v.tensor_copy(out=T.gat[:, 0:128], in_=piece(0)).then_inc(sem.ga0, 1)
    for h in range(H):
        v.wait_ge(sem["ga%d" % h], 1)
        v.transpose(out=T.x[:, 128 * h:128 * h + 128], in_=T.gat[:, 128 * h:128 * h + 128]).then_inc(sem["bk%d" % h], 1)
    for h in range(H - 1):
        sy.wait_ge(sem["bk%d" % h], 1)
        sy.dma_start(T.y[1024 * h:1024 * h + 1024, :], T.x[:, 128 * h:128 * h + 128]).then_inc(sem.st, 16)
    h = H - 1
    act.wait_ge(sem["bk%d" % h], 1)
    act.dma_start(T.y[1024 * h:1024 * h + 1024, :], T.x[:, 128 * h:128 * h + 128]).then_inc(sem.stl, 16)
    sy.wait_ge(sem.st, 16 * (H - 1))
    act.wait_ge(sem.stl, 16)
    g.wait_ge(sem.ls, 2 * 3 * NE)
